import numpy as np
import ml_dtypes


def mxq(x, axis, fmt="e4m3"):
    dtype, down = {"e4m3": (ml_dtypes.float8_e4m3fn, 7), "e5m2": (ml_dtypes.float8_e5m2, 14)}[fmt]
    v = np.moveaxis(np.asarray(x, np.float32).astype(ml_dtypes.bfloat16).astype(np.float64), axis, -1)
    blocks = v.reshape(v.shape[:-1] + (-1, 32))
    amax = np.abs(blocks).max(-1, keepdims=True)
    byte = np.maximum(np.where(amax > 0, np.frexp(amax)[1] - 1 + 127, 0) - down, 1)
    scale = np.exp2(byte - 127.0)
    codes = (blocks / scale).astype(np.float32).astype(dtype).astype(np.float64)
    return np.moveaxis((codes * scale).reshape(v.shape), -1, axis)


WIDE = False


def mx_kscale(k):
    if not WIDE:
        return np.ones(k)
    levels = np.array([10, -10, 5, -5, 0])
    if k % 512:
        return np.exp2(np.random.permutation(np.resize(levels, k // 32))).repeat(32)
    a = np.empty((k // 512, 16))
    for p in range(k // 512):
        a[p, :8] = np.random.permutation(np.resize(levels, 8))
        for g in range(8):
            far = levels[np.abs(levels - a[p, g]) >= 10]
            a[p, g + 8] = far[np.random.randint(len(far))]
    return np.exp2(a.ravel()).repeat(32)


def f64(x):
    return np.asarray(x).astype(np.float64)


def striped8(idx):
    return np.asarray(idx).reshape(8, -1, 16).transpose(0, 2, 1).reshape(128, -1).astype(np.uint16)


def unstriped8(offs):
    return offs.reshape(8, 16, -1).transpose(0, 2, 1).reshape(8, -1).astype(np.int64)


def pick8(x, idx, run):
    r = np.arange(len(x))
    return x[r[:, None], idx[r % (8 * run) // run]]


E2M1 = np.array([0.0, 0.5, 1.0, 1.5, 2.0, 3.0, 4.0, 6.0, -0.0, -0.5, -1.0, -1.5, -2.0, -3.0, -4.0, -6.0])


def pack_weight(w, fmt):
    k, n = w.shape
    w = f64(np.asarray(w, np.float32).astype(ml_dtypes.bfloat16)).reshape(k // 32, 32, n)
    amax = np.abs(w).max(1)
    if fmt == "e4m3":
        byte = np.frexp(amax)[1] - 1 + 127 - 7
    else:
        mant, ex = np.frexp(amax / 6.0)
        byte = np.where(mant > 0.5, ex, ex - 1) + 127
    byte = np.clip(np.where(amax > 0, byte, 1), 1, 254)
    scaled = (w * np.exp2(127.0 - byte)[:, None, :]).reshape(k, n).astype(np.float32)
    by_word = np.ascontiguousarray(scaled.reshape(k // 512, 128, 4, n).transpose(0, 1, 3, 2))
    if fmt == "e4m3":
        words = by_word.astype(ml_dtypes.float8_e4m3fn).view(np.uint8)
    else:
        c = by_word.astype(ml_dtypes.float4_e2m1fn).view(np.uint8) & 0xF
        words = (c[..., 0::2] | (c[..., 1::2] << 4)).reshape(k // 512, 128, 2 * n)
    return np.ascontiguousarray(words), np.ascontiguousarray(byte.astype(np.uint8).reshape(k // 512, 16, n))


def unpack_weight(words, scales, fmt):
    g, _, n = scales.shape
    words = np.ascontiguousarray(words).reshape(g, 128, n, -1)
    if fmt == "e4m3":
        vals = words.view(ml_dtypes.float8_e4m3fn).astype(np.float64)
    else:
        nib = np.empty((g, 128, n, 4), np.uint8)
        nib[..., 0::2] = words & 0xF
        nib[..., 1::2] = words >> 4
        vals = E2M1[nib]
    vals = vals * np.repeat(np.exp2(scales.astype(np.float64) - 127.0), 8, axis=1)[..., None]
    return vals.transpose(0, 1, 3, 2).reshape(g * 512, n)


D, T, I, Q, E = 512, 1024, 512, 512, 256


def setup_inputs():
    n = np.random.standard_normal
    idx = np.stack([np.random.permutation(T)[:I] for _ in range(8)])
    idx2 = np.stack([np.random.permutation(T)[:I] for _ in range(8)])
    idx3 = np.stack([np.random.permutation(T)[:I] for _ in range(8)])
    idx4 = np.stack([np.random.permutation(T)[:I] for _ in range(8)])
    fd = mx_kscale(D)
    fq = mx_kscale(Q)
    keysp = pack_weight(n((D, T)) / fd[:, None], "e2m1")
    mixp = pack_weight(n((Q, E)) * 1.0 / np.sqrt(Q) / fq[:, None], "e4m3")
    return {
        "query": (n((D, Q)) * 1.0 / np.sqrt(D) * fd[:, None]).astype(np.float32),
        "keys_words": keysp[0],
        "keys_scales": keysp[1],
        "rowf": (np.random.uniform(0.5, 2.0, (Q, 1)) * fq[:, None]).astype(np.float32),
        "mix_words": mixp[0],
        "mix_scales": mixp[1],
        "offs": striped8(idx),
        "offs2": striped8(idx2),
        "offs3": striped8(idx3),
        "offs4": striped8(idx4),
    }


def reference(query, keys_words, keys_scales, rowf, mix_words, mix_scales, offs, offs2, offs3, offs4):
    idx = unstriped8(offs)
    idx2 = unstriped8(offs2)
    idx3 = unstriped8(offs3)
    idx4 = unstriped8(offs4)
    keysu = unpack_weight(keys_words, keys_scales, "e2m1")
    mixu = unpack_weight(mix_words, mix_scales, "e4m3")
    queryq = mxq(f64(query), 0, "e4m3")
    a = queryq.T @ keysu
    f1 = np.zeros((Q, T))
    f1[np.arange(Q)[:, None], idx2[np.arange(Q) % 512 // 64]] = pick8(a, idx, 64)
    f2 = np.zeros((Q, T))
    f2[np.arange(Q)[:, None], idx3[np.arange(Q) % 512 // 64]] = pick8(a, idx2, 64)
    c1 = a + f1
    c2 = c1 - f2
    g = pick8(c2, idx4, 64)
    gw = g * f64(rowf)
    gwq = mxq(gw, 0, "e4m3")
    y = mixu.T @ gwq
    return y

@@ -1,0 +1,172 @@
+from contextlib import ExitStack
+
+import concourse.mybir as mybir
+
+D, T, I, Q, E = 512, 1024, 512, 512, 256
+FLOPS = 2 * D * Q * T + 2 * Q * E * I
+
+F32 = mybir.dt.float32
+BF16 = mybir.dt.bfloat16
+I32 = mybir.dt.int32
+U32 = mybir.dt.uint32
+U16 = mybir.dt.uint16
+U8 = mybir.dt.uint8
+FP8X4 = mybir.dt.float8_e4m3fn_x4
+FP4X4 = mybir.dt.float4_e2m1fn_x4
+COPY = mybir.ActivationFunctionType.Copy
+ADD = mybir.AluOpType.add
+SUB = mybir.AluOpType.subtract
+MULT = mybir.AluOpType.mult
+
+P = 128
+PACK = 4
+BANK = 512
+HALF = I // 2
+GROUP = 16
+
+
+def load_scale_rows(nc, plane, rows):
+    for quad in range(4):
+        nc.sync.dma_start(
+            out=plane[32 * quad : 32 * quad + 4, :].bitcast(I32),
+            in_=rows[4 * quad : 4 * quad + 4, :].bitcast(I32),
+        )
+
+
+def tile_attend_passedalong_one_mixed_kernel(
+    tc, query, keys_words, keys_scales, rowf, mix_words, mix_scales, offs, offs2, offs3, offs4, out
+):
+    nc = tc.nc
+    with ExitStack() as ctx:
+        keep = ctx.enter_context(tc.tile_pool(name="keep", bufs=1))
+        psum = ctx.enter_context(tc.psum_pool(name="psum", bufs=1))
+
+        lists = [keep.tile([P, I // GROUP], U16, name="list%d" % n) for n in range(4)]
+        key_codes = keep.tile([P, 2 * T], U8, align_bytes=64, tag="keys_then_picked")
+        key_plane = keep.tile([P, T], U8, align_bytes=64)
+        mix_codes = keep.tile([P, E], U32, align_bytes=64)
+        mix_plane = keep.tile([P, E], U8, align_bytes=64)
+        factors = keep.tile([P, PACK], F32)
+        raw = [keep.tile([P, PACK, Q // 2], F32, name="raw%d" % c) for c in range(2)]
+        f1 = keep.tile([P, T], F32)
+        f2 = keep.tile([P, T], F32)
+
+        nc.vector.memset(key_plane[:].bitcast(I32), 0)
+        nc.vector.memset(f1[:], 0.0)
+        nc.vector.memset(f2[:], 0.0)
+        nc.vector.memset(mix_plane[:].bitcast(I32), 0)
+
+        query_rows = query.rearrange("(p j) q -> p j q", j=PACK)
+        for c in range(2):
+            nc.sync.dma_start(out=raw[c][:], in_=query_rows[:, :, c * (Q // 2) : (c + 1) * (Q // 2)])
+        nc.sync.dma_start(out=key_codes[:].bitcast(I32), in_=keys_words[0].bitcast(I32))
+        load_scale_rows(nc, key_plane, keys_scales[0])
+        for tile, source in zip(lists, (offs, offs2, offs3, offs4)):
+            nc.sync.dma_start(tile[:], source)
+        nc.sync.dma_start(out=factors[:], in_=rowf.rearrange("(p r) o -> p (r o)", r=PACK))
+        nc.sync.dma_start(
+            out=mix_codes[:].bitcast(I32), in_=mix_words[0].rearrange("p n t -> p (n t)").bitcast(I32)
+        )
+        load_scale_rows(nc, mix_plane, mix_scales[0])
+        first, second, third, result = lists
+
+        dealt = keep.tile([P, PACK, P, PACK], BF16, align_bytes=64)
+        dealt_view = dealt[:].rearrange("p r m j -> p m r j")
+        raw_view = [raw[c][:].rearrange("p j (m r) -> p m r j", r=PACK) for c in range(2)]
+        for c in range(2):
+            members = slice(c * P // 2, (c + 1) * P // 2)
+            nc.vector.tensor_copy(out=dealt_view[:, members, 0, :], in_=raw_view[c][:, :, 0, :])
+            nc.scalar.activation(dealt_view[:, members, 1:PACK, :], raw_view[c][:, :, 1:PACK, :], COPY)
+        query_codes = keep.tile([P, Q], U32, align_bytes=64)
+        query_plane = keep.tile([P, Q], U8, align_bytes=64)
+        dealt_flat = dealt[:].rearrange("p r m j -> p (r m j)")
+        for lo, hi in ((0, P), (P, Q)):
+            nc.vector.quantize_mx(
+                out=query_codes[:, lo:hi].bitcast(FP8X4),
+                scales=query_plane[:, lo:hi],
+                in_=dealt_flat[:, PACK * lo : PACK * hi],
+            )
+
+        passed = [keep.tile([P, T], F32, name="c2_%d" % r) for r in range(PACK)]
+        for r in range(PACK):
+            banks = psum.tile([P, T], F32, name="score_banks")
+            scores = keep.tile([P, T], F32, name="scores%d" % r)
+            rows = slice(r * P, (r + 1) * P)
+            for b in range(T // BANK):
+                cols = slice(b * BANK, (b + 1) * BANK)
+                nc.tensor.matmul_mx(
+                    out=banks[:, cols],
+                    lhsT=query_codes[:, rows].bitcast(FP8X4),
+                    lhsT_scale=query_plane[:, rows],
+                    rhs=key_codes[:, 2 * b * BANK : 2 * (b + 1) * BANK].bitcast(FP4X4),
+                    rhs_scale=key_plane[:, cols],
+                    start=True,
+                    stop=True,
+                )
+                nc.scalar.activation(scores[:, cols], banks[:, cols], COPY)
+
+            at_first = keep.tile([P, I], F32, name="at_first%d" % r)
+            at_second = keep.tile([P, I], F32, name="at_second%d" % r)
+            pieces = 2 if r == 0 else 1
+            width = I // pieces
+            for piece in range(pieces):
+                slots = slice(piece * width, (piece + 1) * width)
+                entries = slice(piece * width // GROUP, (piece + 1) * width // GROUP)
+                if r == 0 and piece == 0:
+                    nc.vector.tensor_copy(at_first[:, slots], scores[:].indirect(first[:, entries]))
+                else:
+                    nc.scalar.activation(at_first[:, slots], scores[:].indirect(first[:, entries]), COPY)
+                nc.vector.tensor_copy(f1[:].indirect(second[:, entries]), at_first[:, slots])
+            nc.scalar.activation(at_second[:], scores[:].indirect(second[:]), COPY)
+            nc.vector.tensor_copy(f2[:].indirect(third[:]), at_second[:])
+            nc.gpsimd.tensor_tensor(passed[r][:], scores[:], f1[:], ADD)
+            engine = nc.vector if r == PACK - 1 else nc.gpsimd
+            engine.tensor_tensor(passed[r][:], passed[r][:], f2[:], SUB)
+
+        weighted = keep.tile([P, I, PACK], BF16, align_bytes=64)
+        for r in range(PACK - 1):
+            picked = keep.tile([P, I], F32, name="picked%d" % r, align_bytes=64, tag="keys_then_picked")
+            nc.scalar.activation(picked[:], passed[r][:].indirect(result[:]), COPY)
+            nc.scalar.activation(weighted[:, :, r], picked[:], COPY, scale=factors[:, r : r + 1])
+
+        last = PACK - 1
+        picked_last = keep.tile([P, I], F32, align_bytes=64, tag="keys_then_picked")
+        for h in range(2):
+            slots = slice(h * HALF, (h + 1) * HALF)
+            entries = slice(h * HALF // GROUP, (h + 1) * HALF // GROUP)
+            nc.scalar.activation(picked_last[:, slots], passed[last][:].indirect(result[:, entries]), COPY)
+            nc.vector.tensor_scalar(
+                weighted[:, slots, last], picked_last[:, slots], factors[:, last : last + 1], None, MULT
+            )
+
+        weighted_codes = keep.tile([P, I], U32, align_bytes=64)
+        weighted_plane = keep.tile([P, I], U8, align_bytes=64)
+        weighted_flat = weighted[:].rearrange("p i r -> p (i r)")
+        out_rows = out.rearrange("(x p) i -> p x i", p=P)
+        for h in range(2):
+            slots = slice(h * HALF, (h + 1) * HALF)
+            nc.vector.quantize_mx(
+                out=weighted_codes[:, slots].bitcast(FP8X4),
+                scales=weighted_plane[:, slots],
+                in_=weighted_flat[:, PACK * h * HALF : PACK * (h + 1) * HALF],
+            )
+        for h in range(2):
+            slots = slice(h * HALF, (h + 1) * HALF)
+            staged = keep.tile([P, E // P, HALF], F32, name="staged%d" % h)
+            for x in range(E // P):
+                mixed = psum.tile([P, HALF], F32, name="mixed%d_%d" % (h, x))
+                channels = slice(x * P, (x + 1) * P)
+                nc.tensor.matmul_mx(
+                    out=mixed[:],
+                    lhsT=mix_codes[:, channels].bitcast(FP8X4),
+                    lhsT_scale=mix_plane[:, channels],
+                    rhs=weighted_codes[:, slots].bitcast(FP8X4),
+                    rhs_scale=weighted_plane[:, slots],
+                    start=True,
+                    stop=True,
+                )
+                if x == 0:
+                    nc.scalar.copy(staged[:, x, :], mixed[:])
+                else:
+                    nc.vector.tensor_copy(staged[:, x, :], mixed[:])
+            nc.sync.dma_start(out=out_rows[:, :, slots], in_=staged[:])

@@ -20,7 +20,7 @@ MULT = mybir.AluOpType.mult
 
 P = 128
 PACK = 4
-BANK = 512
+RUN = 256
 HALF = I // 2
 GROUP = 16
 
@@ -47,7 +47,7 @@ def tile_attend_passedalong_one_mixed_kernel(
         mix_codes = keep.tile([P, E], U32, align_bytes=64)
         mix_plane = keep.tile([P, E], U8, align_bytes=64)
         factors = keep.tile([P, PACK], F32)
-        raw = [keep.tile([P, PACK, Q // 2], F32, name="raw%d" % c) for c in range(2)]
+        raw = keep.tile([P, PACK, Q], F32)
         f1 = keep.tile([P, T], F32)
         f2 = keep.tile([P, T], F32)
 
@@ -58,7 +58,7 @@ def tile_attend_passedalong_one_mixed_kernel(
 
         query_rows = query.rearrange("(p j) q -> p j q", j=PACK)
         for c in range(2):
-            nc.sync.dma_start(out=raw[c][:], in_=query_rows[:, :, c * (Q // 2) : (c + 1) * (Q // 2)])
+            nc.sync.dma_start(out=raw[:, 2 * c : 2 * c + 2, :], in_=query_rows[:, 2 * c : 2 * c + 2, :])
         nc.sync.dma_start(out=key_codes[:].bitcast(I32), in_=keys_words[0].bitcast(I32))
         load_scale_rows(nc, key_plane, keys_scales[0])
         for tile, source in zip(lists, (offs, offs2, offs3, offs4)):
@@ -70,40 +70,44 @@ def tile_attend_passedalong_one_mixed_kernel(
         load_scale_rows(nc, mix_plane, mix_scales[0])
         first, second, third, result = lists
 
-        dealt = keep.tile([P, PACK, P, PACK], BF16, align_bytes=64)
-        dealt_view = dealt[:].rearrange("p r m j -> p m r j")
-        raw_view = [raw[c][:].rearrange("p j (m r) -> p m r j", r=PACK) for c in range(2)]
-        for c in range(2):
-            members = slice(c * P // 2, (c + 1) * P // 2)
-            nc.vector.tensor_copy(out=dealt_view[:, members, 0, :], in_=raw_view[c][:, :, 0, :])
-            nc.scalar.activation(dealt_view[:, members, 1:PACK, :], raw_view[c][:, :, 1:PACK, :], COPY)
         query_codes = keep.tile([P, Q], U32, align_bytes=64)
         query_plane = keep.tile([P, Q], U8, align_bytes=64)
-        dealt_flat = dealt[:].rearrange("p r m j -> p (r m j)")
-        for lo, hi in ((0, P), (P, Q)):
-            nc.vector.quantize_mx(
-                out=query_codes[:, lo:hi].bitcast(FP8X4),
-                scales=query_plane[:, lo:hi],
-                in_=dealt_flat[:, PACK * lo : PACK * hi],
+        raw_view = raw[:].rearrange("p j (m r) -> p m r j", r=PACK)
+        dealt_first = keep.tile([P, P, PACK], BF16, align_bytes=64, tag="dealt")
+        for c in range(2):
+            nc.vector.tensor_copy(
+                out=dealt_first[:, :, 2 * c : 2 * c + 2], in_=raw_view[:, :, 0, 2 * c : 2 * c + 2]
             )
+        nc.vector.quantize_mx(
+            out=query_codes[:, 0:P].bitcast(FP8X4),
+            scales=query_plane[:, 0:P],
+            in_=dealt_first[:].rearrange("p m j -> p (m j)"),
+        )
+        dealt_rest = keep.tile([P, PACK - 1, P, PACK], BF16, align_bytes=64, tag="dealt")
+        nc.vector.tensor_copy(out=dealt_rest[:].rearrange("p r m j -> p m r j"), in_=raw_view[:, :, 1:PACK, :])
+        nc.vector.quantize_mx(
+            out=query_codes[:, P:Q].bitcast(FP8X4),
+            scales=query_plane[:, P:Q],
+            in_=dealt_rest[:].rearrange("p r m j -> p (r m j)"),
+        )
 
         passed = [keep.tile([P, T], F32, name="c2_%d" % r) for r in range(PACK)]
         for r in range(PACK):
-            banks = psum.tile([P, T], F32, name="score_banks")
             scores = keep.tile([P, T], F32, name="scores%d" % r)
             rows = slice(r * P, (r + 1) * P)
-            for b in range(T // BANK):
-                cols = slice(b * BANK, (b + 1) * BANK)
+            for b in range(T // RUN):
+                cols = slice(b * RUN, (b + 1) * RUN)
+                bank = psum.tile([P, RUN], F32, name="score_bank%d" % b)
                 nc.tensor.matmul_mx(
-                    out=banks[:, cols],
+                    out=bank[:],
                     lhsT=query_codes[:, rows].bitcast(FP8X4),
                     lhsT_scale=query_plane[:, rows],
-                    rhs=key_codes[:, 2 * b * BANK : 2 * (b + 1) * BANK].bitcast(FP4X4),
+                    rhs=key_codes[:, 2 * b * RUN : 2 * (b + 1) * RUN].bitcast(FP4X4),
                     rhs_scale=key_plane[:, cols],
                     start=True,
                     stop=True,
                 )
-                nc.scalar.activation(scores[:, cols], banks[:, cols], COPY)
+                nc.scalar.activation(scores[:, cols], bank[:], COPY)
 
             at_first = keep.tile([P, I], F32, name="at_first%d" % r)
             at_second = keep.tile([P, I], F32, name="at_second%d" % r)
@@ -134,7 +138,12 @@ def tile_attend_passedalong_one_mixed_kernel(
         for h in range(2):
             slots = slice(h * HALF, (h + 1) * HALF)
             entries = slice(h * HALF // GROUP, (h + 1) * HALF // GROUP)
-            nc.scalar.activation(picked_last[:, slots], passed[last][:].indirect(result[:, entries]), COPY)
+            if h == 0:
+                nc.vector.tensor_copy(picked_last[:, slots], passed[last][:].indirect(result[:, entries]))
+            else:
+                nc.scalar.activation(picked_last[:, slots], passed[last][:].indirect(result[:, entries]), COPY)
+        for h in range(2):
+            slots = slice(h * HALF, (h + 1) * HALF)
             nc.vector.tensor_scalar(
                 weighted[:, slots, last], picked_last[:, slots], factors[:, last : last + 1], None, MULT
             )
@@ -165,8 +174,12 @@ def tile_attend_passedalong_one_mixed_kernel(
                     start=True,
                     stop=True,
                 )
-                if x == 0:
+                if x == 0 or h == 0:
                     nc.scalar.copy(staged[:, x, :], mixed[:])
                 else:
                     nc.vector.tensor_copy(staged[:, x, :], mixed[:])
-            nc.sync.dma_start(out=out_rows[:, :, slots], in_=staged[:])
+            if h == 0:
+                nc.sync.dma_start(out=out_rows[:, :, slots], in_=staged[:])
+            else:
+                nc.scalar.dma_start(out=out_rows[:, 0, slots], in_=staged[:, 0, :])
+                nc.sync.dma_start(out=out_rows[:, 1, slots], in_=staged[:, 1, :])

from contextlib import ExitStack

import concourse.mybir as mybir

D, T, I, Q, E = 512, 1024, 512, 512, 256
FLOPS = 2 * D * Q * T + 2 * Q * E * I

F32 = mybir.dt.float32
BF16 = mybir.dt.bfloat16
I32 = mybir.dt.int32
U32 = mybir.dt.uint32
U16 = mybir.dt.uint16
U8 = mybir.dt.uint8
FP8X4 = mybir.dt.float8_e4m3fn_x4
FP4X4 = mybir.dt.float4_e2m1fn_x4
COPY = mybir.ActivationFunctionType.Copy
ADD = mybir.AluOpType.add
SUB = mybir.AluOpType.subtract
MULT = mybir.AluOpType.mult

P = 128
PACK = 4
RUN = 256
HALF = I // 2
GROUP = 16


def load_scale_rows(nc, plane, rows):
    for quad in range(4):
        nc.sync.dma_start(
            out=plane[32 * quad : 32 * quad + 4, :].bitcast(I32),
            in_=rows[4 * quad : 4 * quad + 4, :].bitcast(I32),
        )


def tile_attend_passedalong_one_mixed_kernel(
    tc, query, keys_words, keys_scales, rowf, mix_words, mix_scales, offs, offs2, offs3, offs4, out
):
    nc = tc.nc
    with ExitStack() as ctx:
        keep = ctx.enter_context(tc.tile_pool(name="keep", bufs=1))
        psum = ctx.enter_context(tc.psum_pool(name="psum", bufs=1))

        lists = [keep.tile([P, I // GROUP], U16, name="list%d" % n) for n in range(4)]
        key_codes = keep.tile([P, 2 * T], U8, align_bytes=64, tag="keys_then_picked")
        key_plane = keep.tile([P, T], U8, align_bytes=64)
        mix_codes = keep.tile([P, E], U32, align_bytes=64)
        mix_plane = keep.tile([P, E], U8, align_bytes=64)
        factors = keep.tile([P, PACK], F32)
        raw = keep.tile([P, PACK, Q], F32)
        f1 = keep.tile([P, T], F32)
        f2 = keep.tile([P, T], F32)

        nc.vector.memset(key_plane[:].bitcast(I32), 0)
        nc.vector.memset(f1[:], 0.0)
        nc.vector.memset(f2[:], 0.0)
        nc.vector.memset(mix_plane[:].bitcast(I32), 0)

        query_rows = query.rearrange("(p j) q -> p j q", j=PACK)
        for c in range(2):
            nc.sync.dma_start(out=raw[:, 2 * c : 2 * c + 2, :], in_=query_rows[:, 2 * c : 2 * c + 2, :])
        nc.sync.dma_start(out=key_codes[:].bitcast(I32), in_=keys_words[0].bitcast(I32))
        load_scale_rows(nc, key_plane, keys_scales[0])
        for tile, source in zip(lists, (offs, offs2, offs3, offs4)):
            nc.sync.dma_start(tile[:], source)
        nc.sync.dma_start(out=factors[:], in_=rowf.rearrange("(p r) o -> p (r o)", r=PACK))
        nc.sync.dma_start(
            out=mix_codes[:].bitcast(I32), in_=mix_words[0].rearrange("p n t -> p (n t)").bitcast(I32)
        )
        load_scale_rows(nc, mix_plane, mix_scales[0])
        first, second, third, result = lists

        query_codes = keep.tile([P, Q], U32, align_bytes=64)
        query_plane = keep.tile([P, Q], U8, align_bytes=64)
        raw_view = raw[:].rearrange("p j (m r) -> p m r j", r=PACK)
        dealt_first = keep.tile([P, P, PACK], BF16, align_bytes=64, tag="dealt")
        for c in range(2):
            nc.vector.tensor_copy(
                out=dealt_first[:, :, 2 * c : 2 * c + 2], in_=raw_view[:, :, 0, 2 * c : 2 * c + 2]
            )
        nc.vector.quantize_mx(
            out=query_codes[:, 0:P].bitcast(FP8X4),
            scales=query_plane[:, 0:P],
            in_=dealt_first[:].rearrange("p m j -> p (m j)"),
        )
        dealt_rest = keep.tile([P, PACK - 1, P, PACK], BF16, align_bytes=64, tag="dealt")
        nc.vector.tensor_copy(out=dealt_rest[:].rearrange("p r m j -> p m r j"), in_=raw_view[:, :, 1:PACK, :])
        nc.vector.quantize_mx(
            out=query_codes[:, P:Q].bitcast(FP8X4),
            scales=query_plane[:, P:Q],
            in_=dealt_rest[:].rearrange("p r m j -> p (r m j)"),
        )

        passed = [keep.tile([P, T], F32, name="c2_%d" % r) for r in range(PACK)]
        for r in range(PACK):
            scores = keep.tile([P, T], F32, name="scores%d" % r)
            rows = slice(r * P, (r + 1) * P)
            for b in range(T // RUN):
                cols = slice(b * RUN, (b + 1) * RUN)
                bank = psum.tile([P, RUN], F32, name="score_bank%d" % b)
                nc.tensor.matmul_mx(
                    out=bank[:],
                    lhsT=query_codes[:, rows].bitcast(FP8X4),
                    lhsT_scale=query_plane[:, rows],
                    rhs=key_codes[:, 2 * b * RUN : 2 * (b + 1) * RUN].bitcast(FP4X4),
                    rhs_scale=key_plane[:, cols],
                    start=True,
                    stop=True,
                )
                nc.scalar.activation(scores[:, cols], bank[:], COPY)

            at_first = keep.tile([P, I], F32, name="at_first%d" % r)
            at_second = keep.tile([P, I], F32, name="at_second%d" % r)
            pieces = 2 if r == 0 else 1
            width = I // pieces
            for piece in range(pieces):
                slots = slice(piece * width, (piece + 1) * width)
                entries = slice(piece * width // GROUP, (piece + 1) * width // GROUP)
                if r == 0 and piece == 0:
                    nc.vector.tensor_copy(at_first[:, slots], scores[:].indirect(first[:, entries]))
                else:
                    nc.scalar.activation(at_first[:, slots], scores[:].indirect(first[:, entries]), COPY)
                nc.vector.tensor_copy(f1[:].indirect(second[:, entries]), at_first[:, slots])
            nc.scalar.activation(at_second[:], scores[:].indirect(second[:]), COPY)
            nc.vector.tensor_copy(f2[:].indirect(third[:]), at_second[:])
            nc.gpsimd.tensor_tensor(passed[r][:], scores[:], f1[:], ADD)
            engine = nc.vector if r == PACK - 1 else nc.gpsimd
            engine.tensor_tensor(passed[r][:], passed[r][:], f2[:], SUB)

        weighted = keep.tile([P, I, PACK], BF16, align_bytes=64)
        for r in range(PACK - 1):
            picked = keep.tile([P, I], F32, name="picked%d" % r, align_bytes=64, tag="keys_then_picked")
            nc.scalar.activation(picked[:], passed[r][:].indirect(result[:]), COPY)
            nc.scalar.activation(weighted[:, :, r], picked[:], COPY, scale=factors[:, r : r + 1])

        last = PACK - 1
        picked_last = keep.tile([P, I], F32, align_bytes=64, tag="keys_then_picked")
        for h in range(2):
            slots = slice(h * HALF, (h + 1) * HALF)
            entries = slice(h * HALF // GROUP, (h + 1) * HALF // GROUP)
            if h == 0:
                nc.vector.tensor_copy(picked_last[:, slots], passed[last][:].indirect(result[:, entries]))
            else:
                nc.scalar.activation(picked_last[:, slots], passed[last][:].indirect(result[:, entries]), COPY)
        for h in range(2):
            slots = slice(h * HALF, (h + 1) * HALF)
            nc.vector.tensor_scalar(
                weighted[:, slots, last], picked_last[:, slots], factors[:, last : last + 1], None, MULT
            )

        weighted_codes = keep.tile([P, I], U32, align_bytes=64)
        weighted_plane = keep.tile([P, I], U8, align_bytes=64)
        weighted_flat = weighted[:].rearrange("p i r -> p (i r)")
        out_rows = out.rearrange("(x p) i -> p x i", p=P)
        for h in range(2):
            slots = slice(h * HALF, (h + 1) * HALF)
            nc.vector.quantize_mx(
                out=weighted_codes[:, slots].bitcast(FP8X4),
                scales=weighted_plane[:, slots],
                in_=weighted_flat[:, PACK * h * HALF : PACK * (h + 1) * HALF],
            )
        for h in range(2):
            slots = slice(h * HALF, (h + 1) * HALF)
            staged = keep.tile([P, E // P, HALF], F32, name="staged%d" % h)
            for x in range(E // P):
                mixed = psum.tile([P, HALF], F32, name="mixed%d_%d" % (h, x))
                channels = slice(x * P, (x + 1) * P)
                nc.tensor.matmul_mx(
                    out=mixed[:],
                    lhsT=mix_codes[:, channels].bitcast(FP8X4),
                    lhsT_scale=mix_plane[:, channels],
                    rhs=weighted_codes[:, slots].bitcast(FP8X4),
                    rhs_scale=weighted_plane[:, slots],
                    start=True,
                    stop=True,
                )
                if x == 0 or h == 0:
                    nc.scalar.copy(staged[:, x, :], mixed[:])
                else:
                    nc.vector.tensor_copy(staged[:, x, :], mixed[:])
            if h == 0:
                nc.sync.dma_start(out=out_rows[:, :, slots], in_=staged[:])
            else:
                nc.scalar.dma_start(out=out_rows[:, 0, slots], in_=staged[:, 0, :])
                nc.sync.dma_start(out=out_rows[:, 1, slots], in_=staged[:, 1, :])
